import numpy as np
import ml_dtypes


def mxq(x, axis, fmt="e4m3"):
    dtype, down = {"e4m3": (ml_dtypes.float8_e4m3fn, 7), "e5m2": (ml_dtypes.float8_e5m2, 14)}[fmt]
    v = np.moveaxis(np.asarray(x, np.float32).astype(ml_dtypes.bfloat16).astype(np.float64), axis, -1)
    blocks = v.reshape(v.shape[:-1] + (-1, 32))
    amax = np.abs(blocks).max(-1, keepdims=True)
    byte = np.maximum(np.where(amax > 0, np.frexp(amax)[1] - 1 + 127, 0) - down, 1)
    scale = np.exp2(byte - 127.0)
    codes = (blocks / scale).astype(np.float32).astype(dtype).astype(np.float64)
    return np.moveaxis((codes * scale).reshape(v.shape), -1, axis)


WIDE = False


def mx_kscale(k, group=512):
    if not WIDE:
        return np.ones(k)
    levels = np.array([18, -18])
    if group != 512:
        return np.exp2(np.random.permutation(np.resize(levels, k // group))).repeat(group)
    if k % 512:
        return np.exp2(np.random.permutation(np.resize(levels, k // 32))).repeat(32)
    a = np.empty((k // 512, 16))
    for p in range(k // 512):
        a[p, :8] = np.random.permutation(np.resize(levels, 8))
        for g in range(8):
            far = levels[np.abs(levels - a[p, g]) >= 10]
            a[p, g + 8] = far[np.random.randint(len(far))]
    return np.exp2(a.ravel()).repeat(32)


def f64(x):
    return np.asarray(x).astype(np.float64)


def bf(x):
    return np.asarray(x, np.float32).astype(ml_dtypes.bfloat16)


def planes(Y):
    r, m = Y.shape
    b = f64(bf(Y)).reshape(r // 32, 32, m)
    amax = np.abs(b).max(1)
    byte = np.clip(np.where(amax > 0, np.frexp(amax)[1] - 1 + 127 - 7, 1), 1, 254)
    codes = (b * np.exp2(127.0 - byte)[:, None, :]).reshape(r, m).astype(np.float32).astype(ml_dtypes.float8_e4m3fn).view(np.uint8)
    words = codes.reshape(r // 512, 128, 4, m).transpose(0, 1, 3, 2)
    return np.ascontiguousarray(words), np.ascontiguousarray(byte.astype(np.uint8).reshape(r // 512, 16, m))


G, D, M, F, O, N = 4, 128, 128, 128, 128, 512


def sgn(shape):
    return np.random.uniform(0.5, 2.0, shape) * np.where(np.random.standard_normal(shape) < 0, -1.0, 1.0)


def setup_inputs():
    n = np.random.standard_normal
    s_d = mx_kscale(D, 0)
    s_f = mx_kscale(F, 0)
    return {
        "x": (n((G, D, N)) * s_d[:, None]).astype(np.float32),
        "w": (n((G, D, M)) / np.sqrt(D) / s_d[:, None]).astype(np.float32),
        "pa": (np.random.uniform(0.05, 0.5, (G, M, 1))).astype(np.float32),
        "hs": (sgn((G, M, 1)) * np.tile(s_f.reshape(F // G, G).T, (1, G))[:, :, None]).astype(np.float32),
        "v": (n((G, F, O)) / np.sqrt(F) / s_f[:, None]).astype(np.float32),
        "cs": (np.random.uniform(0.5, 2.0, (G, O, 1))).astype(np.float32),
        "cb": (0.5 * n((G, O, 1))).astype(np.float32),
    }


def reference(x, w, pa, hs, v, cs, cb):
    wq = mxq(f64(w), 1, "e4m3")
    xq = mxq(f64(x), 1, "e4m3")
    z = wq.transpose(0, 2, 1) @ xq
    h = (np.maximum(z, 0.0) + f64(pa) * np.minimum(z, 0.0)) * f64(hs)
    u = h.reshape(G * M, N).reshape(G, M, N).transpose(1, 0, 2).reshape(G, M, N)
    vq = mxq(f64(v), 1, "e4m3")
    uq = mxq(u, 1, "e4m3")
    y = vq.transpose(0, 2, 1) @ uq
    a = y * f64(cs) + f64(cb)
    Y = a.reshape(G * O, N)
    words, scales = planes(Y)
    return Y, words, scales

@@ -1,0 +1,192 @@
+from contextlib import ExitStack
+
+import concourse.mybir as mybir
+
+G, D, N = 4, 128, 512
+FLOPS = 2 * 2 * G * D * D * N
+
+F32 = mybir.dt.float32
+BF16 = mybir.dt.bfloat16
+I32 = mybir.dt.int32
+U32 = mybir.dt.uint32
+U8 = mybir.dt.uint8
+FP8X4 = mybir.dt.float8_e4m3fn_x4
+ALU = mybir.AluOpType
+IDENT = mybir.ActivationFunctionType.Identity
+
+P = 128
+PACK = 4
+ROWS = 32
+C = 128
+NCH = N // C
+
+
+def tile_rows_pl_monarch_prelu_kernel(tc, x, w, pa, hs, v, cs, cb, out_0, out_1, out_2):
+    nc = tc.nc
+    with ExitStack() as ctx:
+        sb = ctx.enter_context(tc.tile_pool(name="sb", bufs=1))
+        ps = ctx.enter_context(tc.psum_pool(name="ps", bufs=1))
+        ctx.enter_context(tc.manual_schedule())
+
+        def tile(name, shape, dtype):
+            return sb.tile(shape, dtype, name=name, align_bytes=64)
+
+        banks = [[ps.tile([P, 512], F32, name="bank%d_%d" % (g, b)) for b in range(2)] for g in range(G)]
+
+        def interleave(engine, dst, src):
+            d = dst.rearrange("p (c i) t -> p c t i", i=4)
+            s = src.rearrange("p t (c i) -> p c t i", i=4)
+            if engine == "v":
+                nc.vector.tensor_copy(out=d, in_=s)
+            else:
+                nc.scalar.activation(out=d, in_=s, func=IDENT)
+
+        def quantize(codes, scales, grouped):
+            nc.vector.quantize_mx(out=codes.bitcast(FP8X4), scales=scales, in_=grouped.rearrange("p n t -> p (n t)"))
+
+        def products(outs, wc, wsc, ac, asc):
+            for g in range(G):
+                r = slice(ROWS * g, ROWS * (g + 1))
+                nc.tensor.matmul_mx(out=outs[g], lhsT=wc[r, :].bitcast(FP8X4), lhsT_scale=wsc[r, :],
+                                    rhs=ac[r, :].bitcast(FP8X4), rhs_scale=asc[r, :], start=True, stop=True)
+
+        x_rows = x.rearrange("g (p j) n -> (g p) j n", j=PACK)
+        par_rows = tile("par_rows", [P, 32], F32)
+        nc.vector.memset(par_rows[:], 0.0)
+        w_raw = tile("w_raw", [P, PACK, D], F32)
+        v_raw = tile("v_raw", [P, PACK, D], F32)
+        x_raw = [tile("x_raw0", [P, PACK, C], F32), tile("x_raw1", [P, PACK, C], F32), tile("x_raw2", [P, PACK, 2 * C], F32)]
+        nc.sync.dma_start(out=w_raw[:], in_=w.rearrange("g (p j) m -> (g p) j m", j=PACK))
+        nc.sync.dma_start(out=x_raw[0][:], in_=x_rows[:, :, 0:C])
+        for k, vec in enumerate((pa, hs, cs, cb)):
+            nc.sync.dma_start(out=par_rows[k:P:8, :], in_=vec.rearrange("g (q c) o -> q g (c o)", q=4))
+        nc.sync.dma_start(out=x_raw[1][:], in_=x_rows[:, :, C:2 * C])
+        nc.sync.dma_start(out=v_raw[:], in_=v.rearrange("g (p j) m -> (g p) j m", j=PACK))
+        nc.sync.dma_start(out=x_raw[2][:], in_=x_rows[:, :, 2 * C:N])
+        x_src = [x_raw[0][:], x_raw[1][:], x_raw[2][:, :, 0:C], x_raw[2][:, :, C:2 * C]]
+
+        par = tile("par", [P, 32], F32)
+        negd = tile("negd", [P, G], F32)
+        two = tile("two", [P, G], F32)
+        alpha = tile("alpha", [P, G], F32)
+        w_b = tile("w_b", [P, D, PACK], BF16)
+        v_b = tile("v_b", [P, D, PACK], BF16)
+        w_c = tile("w_c", [P, D], U32)
+        w_s = tile("w_s", [P, D], U8)
+        v_c = tile("v_c", [P, D], U32)
+        v_s = tile("v_s", [P, D], U8)
+        x_b = [tile("x_b%d" % c, [P, C, PACK], BF16) for c in range(NCH)]
+        x_c = [tile("x_c%d" % c, [P, C], U32) for c in range(NCH)]
+        x_s = [tile("x_s%d" % c, [P, C], U8) for c in range(NCH)]
+        t_f = [tile("t_f%d" % c, [P, G, C], F32) for c in range(NCH)]
+        h_b = [tile("h_b%d" % c, [P, G, C], BF16) for c in range(NCH)]
+        u_b = [tile("u_b%d" % c, [P, C, PACK], BF16) for c in range(NCH)]
+        u_c = [tile("u_c%d" % c, [P, C], U32) for c in range(NCH)]
+        u_s = [tile("u_s%d" % c, [P, C], U8) for c in range(NCH)]
+        y_f = [tile("y_f%d" % h, [P, G, 2 * C], F32) for h in range(2)]
+        r_f = [tile("r_f%d" % c, [P, PACK, C], F32) for c in range(NCH)]
+        y_b = [tile("y_b%d" % c, [P, C, PACK], BF16) for c in range(NCH)]
+        y_c = tile("y_c", [P, N], I32)
+        y_s = tile("y_s", [P, N], U8)
+        out_rows = out_0.rearrange("(g o) n -> o g n", g=G)
+        words = out_1.rearrange("r p n s -> (r p) (n s)").bitcast(I32)
+        srows = out_2.rearrange("r t n -> (r t) n").bitcast(I32)
+
+        def zreg(c, g):
+            return banks[g][c % 2][:, (c // 2) * C:(c // 2 + 1) * C]
+
+        def yreg(c, g):
+            return banks[g][c % 2][:, (2 + c // 2) * C:(3 + c // 2) * C]
+
+        def XI(c, e):
+            interleave(e, x_b[c][:], x_src[c])
+
+        def XQ(c):
+            quantize(x_c[c][:], x_s[c][:], x_b[c][:])
+            products([zreg(c, g) for g in range(G)], w_c, w_s, x_c[c], x_s[c])
+
+        def A(c):
+            for g in range(G):
+                nc.scalar.activation(out=t_f[c][:, g, :], in_=zreg(c, g), func=IDENT, scale=alpha[:, g:g + 1])
+
+        def PR(c):
+            for g in range(G):
+                nc.vector.scalar_tensor_tensor(out=h_b[c][:, g, :], in0=t_f[c][:, g, :], scalar=par[:, 8 * g:8 * g + 1],
+                                               in1=t_f[c][:, g, :], op0=ALU.mult, op1=ALU.max)
+
+        def UI(c, e):
+            interleave(e, u_b[c][:], h_b[c][:])
+
+        def UQ(c):
+            quantize(u_c[c][:], u_s[c][:], u_b[c][:])
+            products([yreg(c, g) for g in range(G)], v_c, v_s, u_c[c], u_s[c])
+
+        def E(c, engines):
+            for g in (0, 2, 1, 3):
+                dst = y_f[c // 2][:, g, (c % 2) * C:(c % 2 + 1) * C]
+                scale, bias = par[:, 8 * g + 2:8 * g + 3], par[:, 8 * g + 3:8 * g + 4]
+                if engines[g] == "s":
+                    nc.scalar.activation(out=dst, in_=yreg(c, g), func=IDENT, scale=scale, bias=bias)
+                else:
+                    nc.vector.tensor_scalar(out=dst, in0=yreg(c, g), scalar1=scale, scalar2=bias, op0=ALU.mult, op1=ALU.add)
+                nc.sync.dma_start(out=r_f[c][ROWS * g:ROWS * (g + 1), :, :], in_=dst)
+            if c % 2 == 1:
+                h = c // 2
+                nc.sync.dma_start(out=out_rows[:, :, 2 * C * h:2 * C * (h + 1)], in_=y_f[h][:])
+
+        def YI(c, e):
+            interleave(e, y_b[c][:], r_f[c][:])
+
+        def YQ(c):
+            quantize(y_c[:, c * C:(c + 1) * C], y_s[:, c * C:(c + 1) * C], y_b[c][:])
+
+        interleave("v", w_b[:], w_raw[:])
+        XI(0, "v")
+        quantize(w_c[:], w_s[:], w_b[:])
+        nc.vector.transpose(out=par[:], in_=par_rows[:])
+        XQ(0)
+        nc.vector.scalar_tensor_tensor(out=negd[:], in0=par[:, 0:32:8], scalar=1.0, in1=par[:, 1:32:8], op0=ALU.subtract, op1=ALU.mult)
+        nc.vector.tensor_scalar(out=two[:], in0=negd[:], scalar1=0.0, scalar2=2.0, op0=ALU.is_le, op1=ALU.mult)
+        nc.vector.scalar_tensor_tensor(out=alpha[:], in0=two[:], scalar=1.0, in1=par[:, 1:32:8], op0=ALU.subtract, op1=ALU.mult)
+        XI(1, "s")
+        nc.vector.scalar_tensor_tensor(out=v_b[:], in0=two[:].unsqueeze(1).to_broadcast([P, D, PACK]), scalar=1.0,
+                                       in1=v_raw[:].rearrange("p j o -> p o j"), op0=ALU.subtract, op1=ALU.mult)
+        XQ(1)
+        A(0)
+        PR(0)
+        quantize(v_c[:], v_s[:], v_b[:])
+        XI(2, "v")
+        A(1)
+        UI(0, "v")
+        XQ(2)
+        XI(3, "s")
+        UQ(0)
+        PR(1)
+        XQ(3)
+        A(2)
+        UI(1, "v")
+        E(0, "ssss")
+        PR(2)
+        UQ(1)
+        A(3)
+        UI(2, "v")
+        PR(3)
+        UQ(2)
+        E(1, "ssss")
+        UI(3, "v")
+        YI(0, "v")
+        UQ(3)
+        E(2, "ssss")
+        YQ(0)
+        E(3, "ssvv")
+        YI(1, "s")
+        YI(2, "v")
+        YQ(1)
+        YQ(2)
+        nc.sync.dma_start(out=words[:, 0:3 * C], in_=y_c[:, 0:3 * C])
+        YI(3, "v")
+        YQ(3)
+        nc.sync.dma_start(out=words[:, 3 * C:N], in_=y_c[:, 3 * C:N])
+        for q in range(4):
+            eng = nc.scalar if q % 2 == 0 else nc.sync
+            eng.dma_start(out=srows[4 * q:4 * q + 4, :], in_=y_s[32 * q:32 * q + 4, :].bitcast(I32))

@@ -34,8 +34,8 @@ def tile_rows_pl_monarch_prelu_kernel(tc, x, w, pa, hs, v, cs, cb, out_0, out_1,
         banks = [[ps.tile([P, 512], F32, name="bank%d_%d" % (g, b)) for b in range(2)] for g in range(G)]
 
         def interleave(engine, dst, src):
-            d = dst.rearrange("p (c i) t -> p c t i", i=4)
-            s = src.rearrange("p t (c i) -> p c t i", i=4)
+            d = dst.rearrange("p (c i) t -> p c t i", i=2)
+            s = src.rearrange("p t (c i) -> p c t i", i=2)
             if engine == "v":
                 nc.vector.tensor_copy(out=d, in_=s)
             else:
@@ -51,23 +51,27 @@ def tile_rows_pl_monarch_prelu_kernel(tc, x, w, pa, hs, v, cs, cb, out_0, out_1,
                                     rhs=ac[r, :].bitcast(FP8X4), rhs_scale=asc[r, :], start=True, stop=True)
 
         x_rows = x.rearrange("g (p j) n -> (g p) j n", j=PACK)
-        par_rows = tile("par_rows", [P, 32], F32)
+        par_rows = tile("par_rows", [P, 64], F32)
         nc.vector.memset(par_rows[:], 0.0)
         w_raw = tile("w_raw", [P, PACK, D], F32)
         v_raw = tile("v_raw", [P, PACK, D], F32)
         x_raw = [tile("x_raw0", [P, PACK, C], F32), tile("x_raw1", [P, PACK, C], F32), tile("x_raw2", [P, PACK, 2 * C], F32)]
-        nc.sync.dma_start(out=w_raw[:], in_=w.rearrange("g (p j) m -> (g p) j m", j=PACK))
         nc.sync.dma_start(out=x_raw[0][:], in_=x_rows[:, :, 0:C])
-        for k, vec in enumerate((pa, hs, cs, cb)):
-            nc.sync.dma_start(out=par_rows[k:P:8, :], in_=vec.rearrange("g (q c) o -> q g (c o)", q=4))
+        for k, vec in enumerate((pa, hs)):
+            nc.sync.dma_start(out=par_rows[k:P:8, 0:32], in_=vec.rearrange("g (q c) o -> q g (c o)", q=4))
+        nc.sync.dma_start(out=w_raw[:], in_=w.rearrange("g (p j) m -> (g p) j m", j=PACK))
         nc.sync.dma_start(out=x_raw[1][:], in_=x_rows[:, :, C:2 * C])
         nc.sync.dma_start(out=v_raw[:], in_=v.rearrange("g (p j) m -> (g p) j m", j=PACK))
         nc.sync.dma_start(out=x_raw[2][:], in_=x_rows[:, :, 2 * C:N])
+        for k, vec in enumerate((cs, cb)):
+            nc.sync.dma_start(out=par_rows[k:P:8, 32:64], in_=vec.rearrange("g (q c) o -> q g (c o)", q=4))
         x_src = [x_raw[0][:], x_raw[1][:], x_raw[2][:, :, 0:C], x_raw[2][:, :, C:2 * C]]
 
         par = tile("par", [P, 32], F32)
+        par2 = tile("par2", [P, 32], F32)
         negd = tile("negd", [P, G], F32)
         two = tile("two", [P, G], F32)
+        sign = tile("sign", [P, G], F32)
         alpha = tile("alpha", [P, G], F32)
         w_b = tile("w_b", [P, D, PACK], BF16)
         v_b = tile("v_b", [P, D, PACK], BF16)
@@ -83,7 +87,7 @@ def tile_rows_pl_monarch_prelu_kernel(tc, x, w, pa, hs, v, cs, cb, out_0, out_1,
         u_b = [tile("u_b%d" % c, [P, C, PACK], BF16) for c in range(NCH)]
         u_c = [tile("u_c%d" % c, [P, C], U32) for c in range(NCH)]
         u_s = [tile("u_s%d" % c, [P, C], U8) for c in range(NCH)]
-        y_f = [tile("y_f%d" % h, [P, G, 2 * C], F32) for h in range(2)]
+        y_f = tile("y_f", [P, G, N], F32)
         r_f = [tile("r_f%d" % c, [P, PACK, C], F32) for c in range(NCH)]
         y_b = [tile("y_b%d" % c, [P, C, PACK], BF16) for c in range(NCH)]
         y_c = tile("y_c", [P, N], I32)
@@ -93,10 +97,10 @@ def tile_rows_pl_monarch_prelu_kernel(tc, x, w, pa, hs, v, cs, cb, out_0, out_1,
         srows = out_2.rearrange("r t n -> (r t) n").bitcast(I32)
 
         def zreg(c, g):
-            return banks[g][c % 2][:, (c // 2) * C:(c // 2 + 1) * C]
+            return banks[g][0][:, c * C:(c + 1) * C]
 
         def yreg(c, g):
-            return banks[g][c % 2][:, (2 + c // 2) * C:(3 + c // 2) * C]
+            return banks[g][0 if c == NCH - 1 else 1][:, c * C:(c + 1) * C]
 
         def XI(c, e):
             interleave(e, x_b[c][:], x_src[c])
@@ -123,16 +127,13 @@ def tile_rows_pl_monarch_prelu_kernel(tc, x, w, pa, hs, v, cs, cb, out_0, out_1,
 
         def E(c, engines):
             for g in (0, 2, 1, 3):
-                dst = y_f[c // 2][:, g, (c % 2) * C:(c % 2 + 1) * C]
-                scale, bias = par[:, 8 * g + 2:8 * g + 3], par[:, 8 * g + 3:8 * g + 4]
+                dst = y_f[:, g, c * C:(c + 1) * C]
+                scale, bias = par2[:, 8 * g:8 * g + 1], par2[:, 8 * g + 1:8 * g + 2]
                 if engines[g] == "s":
                     nc.scalar.activation(out=dst, in_=yreg(c, g), func=IDENT, scale=scale, bias=bias)
                 else:
                     nc.vector.tensor_scalar(out=dst, in0=yreg(c, g), scalar1=scale, scalar2=bias, op0=ALU.mult, op1=ALU.add)
                 nc.sync.dma_start(out=r_f[c][ROWS * g:ROWS * (g + 1), :, :], in_=dst)
-            if c % 2 == 1:
-                h = c // 2
-                nc.sync.dma_start(out=out_rows[:, :, 2 * C * h:2 * C * (h + 1)], in_=y_f[h][:])
 
         def YI(c, e):
             interleave(e, y_b[c][:], r_f[c][:])
@@ -140,46 +141,52 @@ def tile_rows_pl_monarch_prelu_kernel(tc, x, w, pa, hs, v, cs, cb, out_0, out_1,
         def YQ(c):
             quantize(y_c[:, c * C:(c + 1) * C], y_s[:, c * C:(c + 1) * C], y_b[c][:])
 
-        interleave("v", w_b[:], w_raw[:])
         XI(0, "v")
-        quantize(w_c[:], w_s[:], w_b[:])
-        nc.vector.transpose(out=par[:], in_=par_rows[:])
-        XQ(0)
+        nc.vector.transpose(out=par[:], in_=par_rows[:, 0:32])
+        interleave("s", w_b[:, 80:D, :], w_raw[:, :, 80:D])
+        interleave("v", w_b[:, 0:80, :], w_raw[:, :, 0:80])
         nc.vector.scalar_tensor_tensor(out=negd[:], in0=par[:, 0:32:8], scalar=1.0, in1=par[:, 1:32:8], op0=ALU.subtract, op1=ALU.mult)
+        quantize(x_c[0][:], x_s[0][:], x_b[0][:])
         nc.vector.tensor_scalar(out=two[:], in0=negd[:], scalar1=0.0, scalar2=2.0, op0=ALU.is_le, op1=ALU.mult)
+        quantize(w_c[:], w_s[:], w_b[:])
+        products([zreg(0, g) for g in range(G)], w_c, w_s, x_c[0], x_s[0])
         nc.vector.scalar_tensor_tensor(out=alpha[:], in0=two[:], scalar=1.0, in1=par[:, 1:32:8], op0=ALU.subtract, op1=ALU.mult)
+        nc.vector.tensor_scalar(out=sign[:], in0=two[:], scalar1=1.0, scalar2=None, op0=ALU.subtract)
         XI(1, "s")
-        nc.vector.scalar_tensor_tensor(out=v_b[:], in0=two[:].unsqueeze(1).to_broadcast([P, D, PACK]), scalar=1.0,
-                                       in1=v_raw[:].rearrange("p j o -> p o j"), op0=ALU.subtract, op1=ALU.mult)
-        XQ(1)
         A(0)
+        nc.vector.tensor_tensor(out=v_b[:].rearrange("p (c i) t -> p c t i", i=2), in0=v_raw[:].rearrange("p t (c i) -> p c t i", i=2),
+                                in1=sign[:].unsqueeze(1).unsqueeze(3).to_broadcast([P, D // 2, PACK, 2]), op=ALU.mult)
+        XQ(1)
         PR(0)
-        quantize(v_c[:], v_s[:], v_b[:])
-        XI(2, "v")
         A(1)
+        XI(3, "s")
+        XI(2, "v")
         UI(0, "v")
         XQ(2)
-        XI(3, "s")
+        quantize(v_c[:], v_s[:], v_b[:])
         UQ(0)
-        PR(1)
-        XQ(3)
+        nc.vector.transpose(out=par2[:], in_=par_rows[:, 32:64])
         A(2)
-        UI(1, "v")
+        PR(1)
         E(0, "ssss")
+        nc.sync.dma_start(out=out_rows[:, :, 0:C], in_=y_f[:, :, 0:C])
+        XQ(3)
+        UI(1, "v")
         PR(2)
         UQ(1)
         A(3)
         UI(2, "v")
         PR(3)
-        UQ(2)
         E(1, "ssss")
+        UQ(2)
         UI(3, "v")
-        YI(0, "v")
         UQ(3)
         E(2, "ssss")
-        YQ(0)
         E(3, "ssvv")
-        YI(1, "s")
+        nc.sync.dma_start(out=out_rows[:, :, C:N], in_=y_f[:, :, C:N])
+        YI(0, "v")
+        YI(1, "v")
+        YQ(0)
         YI(2, "v")
         YQ(1)
         YQ(2)

@@ -2,8 +2,8 @@ from contextlib import ExitStack
 
 import concourse.mybir as mybir
 
-G, D, N = 4, 128, 512
-FLOPS = 2 * 2 * G * D * D * N
+GROUPS, WIDTH, COLS = 4, 128, 512
+FLOPS = 2 * 2 * GROUPS * WIDTH * WIDTH * COLS
 
 F32 = mybir.dt.float32
 BF16 = mybir.dt.bfloat16
@@ -12,188 +12,231 @@ U32 = mybir.dt.uint32
 U8 = mybir.dt.uint8
 FP8X4 = mybir.dt.float8_e4m3fn_x4
 ALU = mybir.AluOpType
-IDENT = mybir.ActivationFunctionType.Identity
+IDENTITY = mybir.ActivationFunctionType.Identity
 
 P = 128
 PACK = 4
-ROWS = 32
-C = 128
-NCH = N // C
+TILE_ROWS = WIDTH // PACK
+BANK = 512
+CHUNK = 128
+CHUNKS = COLS // CHUNK
+LAST = CHUNKS - 1
+SQUARE = 32
+STRIDE = SQUARE // GROUPS
+SCALE_ROWS = TILE_ROWS // 8
+W_ON_VECTOR = 80
+VECTOR, SCALAR = "vector", "scalar"
 
 
 def tile_rows_pl_monarch_prelu_kernel(tc, x, w, pa, hs, v, cs, cb, out_0, out_1, out_2):
     nc = tc.nc
     with ExitStack() as ctx:
-        sb = ctx.enter_context(tc.tile_pool(name="sb", bufs=1))
-        ps = ctx.enter_context(tc.psum_pool(name="ps", bufs=1))
+        sbuf = ctx.enter_context(tc.tile_pool(name="sbuf", bufs=1))
+        psum = ctx.enter_context(tc.psum_pool(name="psum", bufs=1))
         ctx.enter_context(tc.manual_schedule())
 
         def tile(name, shape, dtype):
-            return sb.tile(shape, dtype, name=name, align_bytes=64)
+            return sbuf.tile(shape, dtype, name=name, align_bytes=64)
 
-        banks = [[ps.tile([P, 512], F32, name="bank%d_%d" % (g, b)) for b in range(2)] for g in range(G)]
+        def chunk_tiles(name, shape, dtype):
+            return [tile("%s%d" % (name, c), shape, dtype) for c in range(CHUNKS)]
 
-        def interleave(engine, dst, src):
-            d = dst.rearrange("p (c i) t -> p c t i", i=2)
-            s = src.rearrange("p t (c i) -> p c t i", i=2)
-            if engine == "v":
-                nc.vector.tensor_copy(out=d, in_=s)
+        def cols(first, end=None):
+            return slice(first * CHUNK, (first + 1 if end is None else end) * CHUNK)
+
+        banks = [[psum.tile([P, BANK], F32, name="bank%d_%d" % (g, b)) for b in range(2)] for g in range(GROUPS)]
+
+        def interleave(engine, dst, src, run):
+            dst_walk = dst.rearrange("p (c i) t -> p c t i", i=run)
+            src_walk = src.rearrange("p t (c i) -> p c t i", i=run)
+            if engine == VECTOR:
+                nc.vector.tensor_copy(out=dst_walk, in_=src_walk)
             else:
-                nc.scalar.activation(out=d, in_=s, func=IDENT)
+                nc.scalar.activation(out=dst_walk, in_=src_walk, func=IDENTITY)
 
-        def quantize(codes, scales, grouped):
-            nc.vector.quantize_mx(out=codes.bitcast(FP8X4), scales=scales, in_=grouped.rearrange("p n t -> p (n t)"))
+        f32_run, bf16_run = 2, 4
 
-        def products(outs, wc, wsc, ac, asc):
-            for g in range(G):
-                r = slice(ROWS * g, ROWS * (g + 1))
-                nc.tensor.matmul_mx(out=outs[g], lhsT=wc[r, :].bitcast(FP8X4), lhsT_scale=wsc[r, :],
-                                    rhs=ac[r, :].bitcast(FP8X4), rhs_scale=asc[r, :], start=True, stop=True)
+        def quantize(codes, scales, interleaved):
+            nc.vector.quantize_mx(out=codes.bitcast(FP8X4), scales=scales, in_=interleaved.rearrange("p n t -> p (n t)"))
 
+        def products(sums, weight_codes, weight_scales, act_codes, act_scales):
+            for g in range(GROUPS):
+                rows = slice(TILE_ROWS * g, TILE_ROWS * (g + 1))
+                nc.tensor.matmul_mx(out=sums[g], lhsT=weight_codes[rows, :].bitcast(FP8X4), lhsT_scale=weight_scales[rows, :],
+                                    rhs=act_codes[rows, :].bitcast(FP8X4), rhs_scale=act_scales[rows, :], start=True, stop=True)
+
+        vector_rows = tile("vector_rows", [P, 2 * SQUARE], F32)
+        nc.vector.memset(vector_rows[:], 0.0)
+
+        def load_vector_pair(pair, half):
+            for k, vec in enumerate(pair):
+                nc.sync.dma_start(out=vector_rows[k:P:STRIDE, half * SQUARE:(half + 1) * SQUARE],
+                                  in_=vec.rearrange("g (q c) o -> q g (c o)", c=SQUARE))
+
+        w_raw = tile("w_raw", [P, PACK, WIDTH], F32)
+        v_raw = tile("v_raw", [P, PACK, WIDTH], F32)
+        x_raw = [tile("x_raw0", [P, PACK, CHUNK], F32), tile("x_raw1", [P, PACK, CHUNK], F32),
+                 tile("x_raw23", [P, PACK, 2 * CHUNK], F32)]
         x_rows = x.rearrange("g (p j) n -> (g p) j n", j=PACK)
-        par_rows = tile("par_rows", [P, 64], F32)
-        nc.vector.memset(par_rows[:], 0.0)
-        w_raw = tile("w_raw", [P, PACK, D], F32)
-        v_raw = tile("v_raw", [P, PACK, D], F32)
-        x_raw = [tile("x_raw0", [P, PACK, C], F32), tile("x_raw1", [P, PACK, C], F32), tile("x_raw2", [P, PACK, 2 * C], F32)]
-        nc.sync.dma_start(out=x_raw[0][:], in_=x_rows[:, :, 0:C])
-        for k, vec in enumerate((pa, hs)):
-            nc.sync.dma_start(out=par_rows[k:P:8, 0:32], in_=vec.rearrange("g (q c) o -> q g (c o)", q=4))
+        nc.sync.dma_start(out=x_raw[0][:], in_=x_rows[:, :, cols(0)])
+        load_vector_pair((pa, hs), 0)
         nc.sync.dma_start(out=w_raw[:], in_=w.rearrange("g (p j) m -> (g p) j m", j=PACK))
-        nc.sync.dma_start(out=x_raw[1][:], in_=x_rows[:, :, C:2 * C])
-        nc.sync.dma_start(out=v_raw[:], in_=v.rearrange("g (p j) m -> (g p) j m", j=PACK))
-        nc.sync.dma_start(out=x_raw[2][:], in_=x_rows[:, :, 2 * C:N])
-        for k, vec in enumerate((cs, cb)):
-            nc.sync.dma_start(out=par_rows[k:P:8, 32:64], in_=vec.rearrange("g (q c) o -> q g (c o)", q=4))
-        x_src = [x_raw[0][:], x_raw[1][:], x_raw[2][:, :, 0:C], x_raw[2][:, :, C:2 * C]]
+        nc.sync.dma_start(out=x_raw[1][:], in_=x_rows[:, :, cols(1)])
+        nc.sync.dma_start(out=v_raw[:], in_=v.rearrange("g (p j) o -> (g p) j o", j=PACK))
+        nc.sync.dma_start(out=x_raw[2][:], in_=x_rows[:, :, cols(2, CHUNKS)])
+        load_vector_pair((cs, cb), 1)
+        x_chunk = [x_raw[0][:], x_raw[1][:], x_raw[2][:, :, cols(0)], x_raw[2][:, :, cols(1)]]
 
-        par = tile("par", [P, 32], F32)
-        par2 = tile("par2", [P, 32], F32)
-        negd = tile("negd", [P, G], F32)
-        two = tile("two", [P, G], F32)
-        sign = tile("sign", [P, G], F32)
-        alpha = tile("alpha", [P, G], F32)
-        w_b = tile("w_b", [P, D, PACK], BF16)
-        v_b = tile("v_b", [P, D, PACK], BF16)
-        w_c = tile("w_c", [P, D], U32)
-        w_s = tile("w_s", [P, D], U8)
-        v_c = tile("v_c", [P, D], U32)
-        v_s = tile("v_s", [P, D], U8)
-        x_b = [tile("x_b%d" % c, [P, C, PACK], BF16) for c in range(NCH)]
-        x_c = [tile("x_c%d" % c, [P, C], U32) for c in range(NCH)]
-        x_s = [tile("x_s%d" % c, [P, C], U8) for c in range(NCH)]
-        t_f = [tile("t_f%d" % c, [P, G, C], F32) for c in range(NCH)]
-        h_b = [tile("h_b%d" % c, [P, G, C], BF16) for c in range(NCH)]
-        u_b = [tile("u_b%d" % c, [P, C, PACK], BF16) for c in range(NCH)]
-        u_c = [tile("u_c%d" % c, [P, C], U32) for c in range(NCH)]
-        u_s = [tile("u_s%d" % c, [P, C], U8) for c in range(NCH)]
-        y_f = tile("y_f", [P, G, N], F32)
-        r_f = [tile("r_f%d" % c, [P, PACK, C], F32) for c in range(NCH)]
-        y_b = [tile("y_b%d" % c, [P, C, PACK], BF16) for c in range(NCH)]
-        y_c = tile("y_c", [P, N], I32)
-        y_s = tile("y_s", [P, N], U8)
-        out_rows = out_0.rearrange("(g o) n -> o g n", g=G)
-        words = out_1.rearrange("r p n s -> (r p) (n s)").bitcast(I32)
-        srows = out_2.rearrange("r t n -> (r t) n").bitcast(I32)
+        pa_hs = tile("pa_hs", [P, SQUARE], F32)
+        cs_cb = tile("cs_cb", [P, SQUARE], F32)
+        pa_all, hs_all = pa_hs[:, 0:SQUARE:STRIDE], pa_hs[:, 1:SQUARE:STRIDE]
+        bend = tile("bend", [P, GROUPS], F32)
+        sign_plus_1 = tile("sign_plus_1", [P, GROUPS], F32)
+        sign = tile("sign", [P, GROUPS], F32)
+        signed_hs = tile("signed_hs", [P, GROUPS], F32)
+        w_bf = tile("w_bf", [P, WIDTH, PACK], BF16)
+        v_bf = tile("v_bf", [P, WIDTH, PACK], BF16)
+        w_codes = tile("w_codes", [P, WIDTH], U32)
+        w_scales = tile("w_scales", [P, WIDTH], U8)
+        v_codes = tile("v_codes", [P, WIDTH], U32)
+        v_scales = tile("v_scales", [P, WIDTH], U8)
+        x_bf = chunk_tiles("x_bf", [P, CHUNK, PACK], BF16)
+        x_codes = chunk_tiles("x_codes", [P, CHUNK], U32)
+        x_scales = chunk_tiles("x_scales", [P, CHUNK], U8)
+        t_f32 = chunk_tiles("t_f32", [P, GROUPS, CHUNK], F32)
+        h_bf = chunk_tiles("h_bf", [P, GROUPS, CHUNK], BF16)
+        u_bf = chunk_tiles("u_bf", [P, CHUNK, PACK], BF16)
+        u_codes = chunk_tiles("u_codes", [P, CHUNK], U32)
+        u_scales = chunk_tiles("u_scales", [P, CHUNK], U8)
+        result = tile("result", [P, GROUPS, COLS], F32)
+        regrouped = chunk_tiles("regrouped", [P, PACK, CHUNK], F32)
+        result_bf = chunk_tiles("result_bf", [P, CHUNK, PACK], BF16)
+        plane_words = tile("plane_words", [P, COLS], I32)
+        plane_scales = tile("plane_scales", [P, COLS], U8)
+        out_rows = out_0.rearrange("(g o) n -> o g n", g=GROUPS)
+        out_words = out_1.rearrange("r p n s -> (r p) (n s)").bitcast(I32)
+        out_scales = out_2.rearrange("r t n -> (r t) n").bitcast(I32)
 
-        def zreg(c, g):
-            return banks[g][0][:, c * C:(c + 1) * C]
+        def z_sums(c, g):
+            return banks[g][0][:, cols(c)]
 
-        def yreg(c, g):
-            return banks[g][0 if c == NCH - 1 else 1][:, c * C:(c + 1) * C]
+        def y_sums(c, g):
+            return banks[g][0 if c == LAST else 1][:, cols(c)]
 
-        def XI(c, e):
-            interleave(e, x_b[c][:], x_src[c])
+        def column(turned, g, k):
+            return turned[:, STRIDE * g + k:STRIDE * g + k + 1]
 
-        def XQ(c):
-            quantize(x_c[c][:], x_s[c][:], x_b[c][:])
-            products([zreg(c, g) for g in range(G)], w_c, w_s, x_c[c], x_s[c])
+        def interleave_x(c, engine):
+            interleave(engine, x_bf[c][:], x_chunk[c], f32_run)
 
-        def A(c):
-            for g in range(G):
-                nc.scalar.activation(out=t_f[c][:, g, :], in_=zreg(c, g), func=IDENT, scale=alpha[:, g:g + 1])
+        def quantize_x(c):
+            quantize(x_codes[c][:], x_scales[c][:], x_bf[c][:])
 
-        def PR(c):
-            for g in range(G):
-                nc.vector.scalar_tensor_tensor(out=h_b[c][:, g, :], in0=t_f[c][:, g, :], scalar=par[:, 8 * g:8 * g + 1],
-                                               in1=t_f[c][:, g, :], op0=ALU.mult, op1=ALU.max)
+        def first_products(c):
+            products([z_sums(c, g) for g in range(GROUPS)], w_codes, w_scales, x_codes[c], x_scales[c])
 
-        def UI(c, e):
-            interleave(e, u_b[c][:], h_b[c][:])
+        def scale_z(c):
+            for g in range(GROUPS):
+                nc.scalar.activation(out=t_f32[c][:, g, :], in_=z_sums(c, g), func=IDENTITY, scale=signed_hs[:, g:g + 1])
 
-        def UQ(c):
-            quantize(u_c[c][:], u_s[c][:], u_b[c][:])
-            products([yreg(c, g) for g in range(G)], v_c, v_s, u_c[c], u_s[c])
+        def prelu(c):
+            for g in range(GROUPS):
+                nc.vector.scalar_tensor_tensor(out=h_bf[c][:, g, :], in0=t_f32[c][:, g, :], scalar=column(pa_hs, g, 0),
+                                               in1=t_f32[c][:, g, :], op0=ALU.mult, op1=ALU.max)
 
-        def E(c, engines):
+        def shuffle(c):
+            interleave(VECTOR, u_bf[c][:], h_bf[c][:], bf16_run)
+
+        def quantize_u_and_multiply(c):
+            quantize(u_codes[c][:], u_scales[c][:], u_bf[c][:])
+            products([y_sums(c, g) for g in range(GROUPS)], v_codes, v_scales, u_codes[c], u_scales[c])
+
+        def finish_and_regroup(c, groups_on_vector=()):
             for g in (0, 2, 1, 3):
-                dst = y_f[:, g, c * C:(c + 1) * C]
-                scale, bias = par2[:, 8 * g:8 * g + 1], par2[:, 8 * g + 1:8 * g + 2]
-                if engines[g] == "s":
-                    nc.scalar.activation(out=dst, in_=yreg(c, g), func=IDENT, scale=scale, bias=bias)
+                values = result[:, g, cols(c)]
+                factor, bias = column(cs_cb, g, 0), column(cs_cb, g, 1)
+                if g in groups_on_vector:
+                    nc.vector.tensor_scalar(out=values, in0=y_sums(c, g), scalar1=factor, scalar2=bias, op0=ALU.mult, op1=ALU.add)
                 else:
-                    nc.vector.tensor_scalar(out=dst, in0=yreg(c, g), scalar1=scale, scalar2=bias, op0=ALU.mult, op1=ALU.add)
-                nc.sync.dma_start(out=r_f[c][ROWS * g:ROWS * (g + 1), :, :], in_=dst)
+                    nc.scalar.activation(out=values, in_=y_sums(c, g), func=IDENTITY, scale=factor, bias=bias)
+                nc.sync.dma_start(out=regrouped[c][TILE_ROWS * g:TILE_ROWS * (g + 1), :, :], in_=values)
 
-        def YI(c, e):
-            interleave(e, y_b[c][:], r_f[c][:])
+        def store_result(columns):
+            nc.sync.dma_start(out=out_rows[:, :, columns], in_=result[:, :, columns])
 
-        def YQ(c):
-            quantize(y_c[:, c * C:(c + 1) * C], y_s[:, c * C:(c + 1) * C], y_b[c][:])
+        def interleave_result(c):
+            interleave(VECTOR, result_bf[c][:], regrouped[c][:], f32_run)
 
-        XI(0, "v")
-        nc.vector.transpose(out=par[:], in_=par_rows[:, 0:32])
-        interleave("s", w_b[:, 80:D, :], w_raw[:, :, 80:D])
-        interleave("v", w_b[:, 0:80, :], w_raw[:, :, 0:80])
-        nc.vector.scalar_tensor_tensor(out=negd[:], in0=par[:, 0:32:8], scalar=1.0, in1=par[:, 1:32:8], op0=ALU.subtract, op1=ALU.mult)
-        quantize(x_c[0][:], x_s[0][:], x_b[0][:])
-        nc.vector.tensor_scalar(out=two[:], in0=negd[:], scalar1=0.0, scalar2=2.0, op0=ALU.is_le, op1=ALU.mult)
-        quantize(w_c[:], w_s[:], w_b[:])
-        products([zreg(0, g) for g in range(G)], w_c, w_s, x_c[0], x_s[0])
-        nc.vector.scalar_tensor_tensor(out=alpha[:], in0=two[:], scalar=1.0, in1=par[:, 1:32:8], op0=ALU.subtract, op1=ALU.mult)
-        nc.vector.tensor_scalar(out=sign[:], in0=two[:], scalar1=1.0, scalar2=None, op0=ALU.subtract)
-        XI(1, "s")
-        A(0)
-        nc.vector.tensor_tensor(out=v_b[:].rearrange("p (c i) t -> p c t i", i=2), in0=v_raw[:].rearrange("p t (c i) -> p c t i", i=2),
-                                in1=sign[:].unsqueeze(1).unsqueeze(3).to_broadcast([P, D // 2, PACK, 2]), op=ALU.mult)
-        XQ(1)
-        PR(0)
-        A(1)
-        XI(3, "s")
-        XI(2, "v")
-        UI(0, "v")
-        XQ(2)
-        quantize(v_c[:], v_s[:], v_b[:])
-        UQ(0)
-        nc.vector.transpose(out=par2[:], in_=par_rows[:, 32:64])
-        A(2)
-        PR(1)
-        E(0, "ssss")
-        nc.sync.dma_start(out=out_rows[:, :, 0:C], in_=y_f[:, :, 0:C])
-        XQ(3)
-        UI(1, "v")
-        PR(2)
-        UQ(1)
-        A(3)
-        UI(2, "v")
-        PR(3)
-        E(1, "ssss")
-        UQ(2)
-        UI(3, "v")
-        UQ(3)
-        E(2, "ssss")
-        E(3, "ssvv")
-        nc.sync.dma_start(out=out_rows[:, :, C:N], in_=y_f[:, :, C:N])
-        YI(0, "v")
-        YI(1, "v")
-        YQ(0)
-        YI(2, "v")
-        YQ(1)
-        YQ(2)
-        nc.sync.dma_start(out=words[:, 0:3 * C], in_=y_c[:, 0:3 * C])
-        YI(3, "v")
-        YQ(3)
-        nc.sync.dma_start(out=words[:, 3 * C:N], in_=y_c[:, 3 * C:N])
-        for q in range(4):
-            eng = nc.scalar if q % 2 == 0 else nc.sync
-            eng.dma_start(out=srows[4 * q:4 * q + 4, :], in_=y_s[32 * q:32 * q + 4, :].bitcast(I32))
+        def quantize_result(c):
+            quantize(plane_words[:, cols(c)], plane_scales[:, cols(c)], result_bf[c][:])
+
+        def store_words(columns):
+            nc.sync.dma_start(out=out_words[:, columns], in_=plane_words[:, columns])
+
+
+        interleave_x(0, VECTOR)
+        nc.vector.transpose(out=pa_hs[:], in_=vector_rows[:, 0:SQUARE])
+        interleave(SCALAR, w_bf[:, W_ON_VECTOR:WIDTH, :], w_raw[:, :, W_ON_VECTOR:WIDTH], f32_run)
+        interleave(VECTOR, w_bf[:, 0:W_ON_VECTOR, :], w_raw[:, :, 0:W_ON_VECTOR], f32_run)
+        nc.vector.scalar_tensor_tensor(out=bend[:], in0=pa_all, scalar=1.0, in1=hs_all, op0=ALU.subtract, op1=ALU.mult)
+        quantize_x(0)
+        nc.vector.tensor_scalar(out=sign_plus_1[:], in0=bend[:], scalar1=0.0, scalar2=2.0, op0=ALU.is_le, op1=ALU.mult)
+        quantize(w_codes[:], w_scales[:], w_bf[:])
+        first_products(0)
+        nc.vector.scalar_tensor_tensor(out=signed_hs[:], in0=sign_plus_1[:], scalar=1.0, in1=hs_all, op0=ALU.subtract, op1=ALU.mult)
+        nc.vector.tensor_scalar(out=sign[:], in0=sign_plus_1[:], scalar1=1.0, scalar2=None, op0=ALU.subtract)
+        interleave_x(1, SCALAR)
+        scale_z(0)
+
+        nc.vector.tensor_tensor(out=v_bf[:].rearrange("p (c i) t -> p c t i", i=f32_run),
+                                in0=v_raw[:].rearrange("p t (c i) -> p c t i", i=f32_run),
+                                in1=sign[:].unsqueeze(1).unsqueeze(3).to_broadcast([P, WIDTH // f32_run, PACK, f32_run]),
+                                op=ALU.mult)
+        quantize_x(1)
+        first_products(1)
+
+        prelu(0)
+        scale_z(1)
+        interleave_x(3, SCALAR)
+        interleave_x(2, VECTOR)
+        shuffle(0)
+        quantize_x(2)
+        first_products(2)
+        quantize(v_codes[:], v_scales[:], v_bf[:])
+        quantize_u_and_multiply(0)
+        nc.vector.transpose(out=cs_cb[:], in_=vector_rows[:, SQUARE:2 * SQUARE])
+        scale_z(2)
+        prelu(1)
+        finish_and_regroup(0)
+        store_result(cols(0))
+        quantize_x(3)
+        first_products(3)
+
+        shuffle(1)
+        prelu(2)
+        quantize_u_and_multiply(1)
+        scale_z(3)
+        shuffle(2)
+        prelu(3)
+        finish_and_regroup(1)
+        quantize_u_and_multiply(2)
+        shuffle(3)
+        quantize_u_and_multiply(3)
+        finish_and_regroup(2)
+        finish_and_regroup(LAST, groups_on_vector=(2, 3))
+
+        store_result(cols(1, CHUNKS))
+        interleave_result(0)
+        interleave_result(1)
+        quantize_result(0)
+        interleave_result(2)
+        quantize_result(1)
+        quantize_result(2)
+        store_words(cols(0, LAST))
+        interleave_result(LAST)
+        quantize_result(LAST)
+        store_words(cols(LAST))
+        for q in range(GROUPS):
+            queue = nc.scalar if q % 2 == 0 else nc.sync
+            queue.dma_start(out=out_scales[SCALE_ROWS * q:SCALE_ROWS * (q + 1), :],
+                            in_=plane_scales[TILE_ROWS * q:TILE_ROWS * q + SCALE_ROWS, :].bitcast(I32))

from contextlib import ExitStack

import concourse.mybir as mybir

GROUPS, WIDTH, COLS = 4, 128, 512
FLOPS = 2 * 2 * GROUPS * WIDTH * WIDTH * COLS

F32 = mybir.dt.float32
BF16 = mybir.dt.bfloat16
I32 = mybir.dt.int32
U32 = mybir.dt.uint32
U8 = mybir.dt.uint8
FP8X4 = mybir.dt.float8_e4m3fn_x4
ALU = mybir.AluOpType
IDENTITY = mybir.ActivationFunctionType.Identity

P = 128
PACK = 4
TILE_ROWS = WIDTH // PACK
BANK = 512
CHUNK = 128
CHUNKS = COLS // CHUNK
LAST = CHUNKS - 1
SQUARE = 32
STRIDE = SQUARE // GROUPS
SCALE_ROWS = TILE_ROWS // 8
W_ON_VECTOR = 80
VECTOR, SCALAR = "vector", "scalar"


def tile_rows_pl_monarch_prelu_kernel(tc, x, w, pa, hs, v, cs, cb, out_0, out_1, out_2):
    nc = tc.nc
    with ExitStack() as ctx:
        sbuf = ctx.enter_context(tc.tile_pool(name="sbuf", bufs=1))
        psum = ctx.enter_context(tc.psum_pool(name="psum", bufs=1))
        ctx.enter_context(tc.manual_schedule())

        def tile(name, shape, dtype):
            return sbuf.tile(shape, dtype, name=name, align_bytes=64)

        def chunk_tiles(name, shape, dtype):
            return [tile("%s%d" % (name, c), shape, dtype) for c in range(CHUNKS)]

        def cols(first, end=None):
            return slice(first * CHUNK, (first + 1 if end is None else end) * CHUNK)

        banks = [[psum.tile([P, BANK], F32, name="bank%d_%d" % (g, b)) for b in range(2)] for g in range(GROUPS)]

        def interleave(engine, dst, src, run):
            dst_walk = dst.rearrange("p (c i) t -> p c t i", i=run)
            src_walk = src.rearrange("p t (c i) -> p c t i", i=run)
            if engine == VECTOR:
                nc.vector.tensor_copy(out=dst_walk, in_=src_walk)
            else:
                nc.scalar.activation(out=dst_walk, in_=src_walk, func=IDENTITY)

        f32_run, bf16_run = 2, 4

        def quantize(codes, scales, interleaved):
            nc.vector.quantize_mx(out=codes.bitcast(FP8X4), scales=scales, in_=interleaved.rearrange("p n t -> p (n t)"))

        def products(sums, weight_codes, weight_scales, act_codes, act_scales):
            for g in range(GROUPS):
                rows = slice(TILE_ROWS * g, TILE_ROWS * (g + 1))
                nc.tensor.matmul_mx(out=sums[g], lhsT=weight_codes[rows, :].bitcast(FP8X4), lhsT_scale=weight_scales[rows, :],
                                    rhs=act_codes[rows, :].bitcast(FP8X4), rhs_scale=act_scales[rows, :], start=True, stop=True)

        vector_rows = tile("vector_rows", [P, 2 * SQUARE], F32)
        nc.vector.memset(vector_rows[:], 0.0)

        def load_vector_pair(pair, half):
            for k, vec in enumerate(pair):
                nc.sync.dma_start(out=vector_rows[k:P:STRIDE, half * SQUARE:(half + 1) * SQUARE],
                                  in_=vec.rearrange("g (q c) o -> q g (c o)", c=SQUARE))

        w_raw = tile("w_raw", [P, PACK, WIDTH], F32)
        v_raw = tile("v_raw", [P, PACK, WIDTH], F32)
        x_raw = [tile("x_raw0", [P, PACK, CHUNK], F32), tile("x_raw1", [P, PACK, CHUNK], F32),
                 tile("x_raw23", [P, PACK, 2 * CHUNK], F32)]
        x_rows = x.rearrange("g (p j) n -> (g p) j n", j=PACK)
        nc.sync.dma_start(out=x_raw[0][:], in_=x_rows[:, :, cols(0)])
        load_vector_pair((pa, hs), 0)
        nc.sync.dma_start(out=w_raw[:], in_=w.rearrange("g (p j) m -> (g p) j m", j=PACK))
        nc.sync.dma_start(out=x_raw[1][:], in_=x_rows[:, :, cols(1)])
        nc.sync.dma_start(out=v_raw[:], in_=v.rearrange("g (p j) o -> (g p) j o", j=PACK))
        nc.sync.dma_start(out=x_raw[2][:], in_=x_rows[:, :, cols(2, CHUNKS)])
        load_vector_pair((cs, cb), 1)
        x_chunk = [x_raw[0][:], x_raw[1][:], x_raw[2][:, :, cols(0)], x_raw[2][:, :, cols(1)]]

        pa_hs = tile("pa_hs", [P, SQUARE], F32)
        cs_cb = tile("cs_cb", [P, SQUARE], F32)
        pa_all, hs_all = pa_hs[:, 0:SQUARE:STRIDE], pa_hs[:, 1:SQUARE:STRIDE]
        bend = tile("bend", [P, GROUPS], F32)
        sign_plus_1 = tile("sign_plus_1", [P, GROUPS], F32)
        sign = tile("sign", [P, GROUPS], F32)
        signed_hs = tile("signed_hs", [P, GROUPS], F32)
        w_bf = tile("w_bf", [P, WIDTH, PACK], BF16)
        v_bf = tile("v_bf", [P, WIDTH, PACK], BF16)
        w_codes = tile("w_codes", [P, WIDTH], U32)
        w_scales = tile("w_scales", [P, WIDTH], U8)
        v_codes = tile("v_codes", [P, WIDTH], U32)
        v_scales = tile("v_scales", [P, WIDTH], U8)
        x_bf = chunk_tiles("x_bf", [P, CHUNK, PACK], BF16)
        x_codes = chunk_tiles("x_codes", [P, CHUNK], U32)
        x_scales = chunk_tiles("x_scales", [P, CHUNK], U8)
        t_f32 = chunk_tiles("t_f32", [P, GROUPS, CHUNK], F32)
        h_bf = chunk_tiles("h_bf", [P, GROUPS, CHUNK], BF16)
        u_bf = chunk_tiles("u_bf", [P, CHUNK, PACK], BF16)
        u_codes = chunk_tiles("u_codes", [P, CHUNK], U32)
        u_scales = chunk_tiles("u_scales", [P, CHUNK], U8)
        result = tile("result", [P, GROUPS, COLS], F32)
        regrouped = chunk_tiles("regrouped", [P, PACK, CHUNK], F32)
        result_bf = chunk_tiles("result_bf", [P, CHUNK, PACK], BF16)
        plane_words = tile("plane_words", [P, COLS], I32)
        plane_scales = tile("plane_scales", [P, COLS], U8)
        out_rows = out_0.rearrange("(g o) n -> o g n", g=GROUPS)
        out_words = out_1.rearrange("r p n s -> (r p) (n s)").bitcast(I32)
        out_scales = out_2.rearrange("r t n -> (r t) n").bitcast(I32)

        def z_sums(c, g):
            return banks[g][0][:, cols(c)]

        def y_sums(c, g):
            return banks[g][0 if c == LAST else 1][:, cols(c)]

        def column(turned, g, k):
            return turned[:, STRIDE * g + k:STRIDE * g + k + 1]

        def interleave_x(c, engine):
            interleave(engine, x_bf[c][:], x_chunk[c], f32_run)

        def quantize_x(c):
            quantize(x_codes[c][:], x_scales[c][:], x_bf[c][:])

        def first_products(c):
            products([z_sums(c, g) for g in range(GROUPS)], w_codes, w_scales, x_codes[c], x_scales[c])

        def scale_z(c):
            for g in range(GROUPS):
                nc.scalar.activation(out=t_f32[c][:, g, :], in_=z_sums(c, g), func=IDENTITY, scale=signed_hs[:, g:g + 1])

        def prelu(c):
            for g in range(GROUPS):
                nc.vector.scalar_tensor_tensor(out=h_bf[c][:, g, :], in0=t_f32[c][:, g, :], scalar=column(pa_hs, g, 0),
                                               in1=t_f32[c][:, g, :], op0=ALU.mult, op1=ALU.max)

        def shuffle(c):
            interleave(VECTOR, u_bf[c][:], h_bf[c][:], bf16_run)

        def quantize_u_and_multiply(c):
            quantize(u_codes[c][:], u_scales[c][:], u_bf[c][:])
            products([y_sums(c, g) for g in range(GROUPS)], v_codes, v_scales, u_codes[c], u_scales[c])

        def finish_and_regroup(c, groups_on_vector=()):
            for g in (0, 2, 1, 3):
                values = result[:, g, cols(c)]
                factor, bias = column(cs_cb, g, 0), column(cs_cb, g, 1)
                if g in groups_on_vector:
                    nc.vector.tensor_scalar(out=values, in0=y_sums(c, g), scalar1=factor, scalar2=bias, op0=ALU.mult, op1=ALU.add)
                else:
                    nc.scalar.activation(out=values, in_=y_sums(c, g), func=IDENTITY, scale=factor, bias=bias)
                nc.sync.dma_start(out=regrouped[c][TILE_ROWS * g:TILE_ROWS * (g + 1), :, :], in_=values)

        def store_result(columns):
            nc.sync.dma_start(out=out_rows[:, :, columns], in_=result[:, :, columns])

        def interleave_result(c):
            interleave(VECTOR, result_bf[c][:], regrouped[c][:], f32_run)

        def quantize_result(c):
            quantize(plane_words[:, cols(c)], plane_scales[:, cols(c)], result_bf[c][:])

        def store_words(columns):
            nc.sync.dma_start(out=out_words[:, columns], in_=plane_words[:, columns])


        interleave_x(0, VECTOR)
        nc.vector.transpose(out=pa_hs[:], in_=vector_rows[:, 0:SQUARE])
        interleave(SCALAR, w_bf[:, W_ON_VECTOR:WIDTH, :], w_raw[:, :, W_ON_VECTOR:WIDTH], f32_run)
        interleave(VECTOR, w_bf[:, 0:W_ON_VECTOR, :], w_raw[:, :, 0:W_ON_VECTOR], f32_run)
        nc.vector.scalar_tensor_tensor(out=bend[:], in0=pa_all, scalar=1.0, in1=hs_all, op0=ALU.subtract, op1=ALU.mult)
        quantize_x(0)
        nc.vector.tensor_scalar(out=sign_plus_1[:], in0=bend[:], scalar1=0.0, scalar2=2.0, op0=ALU.is_le, op1=ALU.mult)
        quantize(w_codes[:], w_scales[:], w_bf[:])
        first_products(0)
        nc.vector.scalar_tensor_tensor(out=signed_hs[:], in0=sign_plus_1[:], scalar=1.0, in1=hs_all, op0=ALU.subtract, op1=ALU.mult)
        nc.vector.tensor_scalar(out=sign[:], in0=sign_plus_1[:], scalar1=1.0, scalar2=None, op0=ALU.subtract)
        interleave_x(1, SCALAR)
        scale_z(0)

        nc.vector.tensor_tensor(out=v_bf[:].rearrange("p (c i) t -> p c t i", i=f32_run),
                                in0=v_raw[:].rearrange("p t (c i) -> p c t i", i=f32_run),
                                in1=sign[:].unsqueeze(1).unsqueeze(3).to_broadcast([P, WIDTH // f32_run, PACK, f32_run]),
                                op=ALU.mult)
        quantize_x(1)
        first_products(1)

        prelu(0)
        scale_z(1)
        interleave_x(3, SCALAR)
        interleave_x(2, VECTOR)
        shuffle(0)
        quantize_x(2)
        first_products(2)
        quantize(v_codes[:], v_scales[:], v_bf[:])
        quantize_u_and_multiply(0)
        nc.vector.transpose(out=cs_cb[:], in_=vector_rows[:, SQUARE:2 * SQUARE])
        scale_z(2)
        prelu(1)
        finish_and_regroup(0)
        store_result(cols(0))
        quantize_x(3)
        first_products(3)

        shuffle(1)
        prelu(2)
        quantize_u_and_multiply(1)
        scale_z(3)
        shuffle(2)
        prelu(3)
        finish_and_regroup(1)
        quantize_u_and_multiply(2)
        shuffle(3)
        quantize_u_and_multiply(3)
        finish_and_regroup(2)
        finish_and_regroup(LAST, groups_on_vector=(2, 3))

        store_result(cols(1, CHUNKS))
        interleave_result(0)
        interleave_result(1)
        quantize_result(0)
        interleave_result(2)
        quantize_result(1)
        quantize_result(2)
        store_words(cols(0, LAST))
        interleave_result(LAST)
        quantize_result(LAST)
        store_words(cols(LAST))
        for q in range(GROUPS):
            queue = nc.scalar if q % 2 == 0 else nc.sync
            queue.dma_start(out=out_scales[SCALE_ROWS * q:SCALE_ROWS * (q + 1), :],
                            in_=plane_scales[TILE_ROWS * q:TILE_ROWS * q + SCALE_ROWS, :].bitcast(I32))
